import numpy as np
import ml_dtypes


def mxq(x, axis, fmt="e4m3"):
    dtype, down = {"e4m3": (ml_dtypes.float8_e4m3fn, 7), "e5m2": (ml_dtypes.float8_e5m2, 14)}[fmt]
    v = np.moveaxis(np.asarray(x, np.float32).astype(ml_dtypes.bfloat16).astype(np.float64), axis, -1)
    blocks = v.reshape(v.shape[:-1] + (-1, 32))
    amax = np.abs(blocks).max(-1, keepdims=True)
    byte = np.maximum(np.where(amax > 0, np.frexp(amax)[1] - 1 + 127, 0) - down, 1)
    scale = np.exp2(byte - 127.0)
    codes = (blocks / scale).astype(np.float32).astype(dtype).astype(np.float64)
    return np.moveaxis((codes * scale).reshape(v.shape), -1, axis)


WIDE = False


def mx_kscale(k):
    if not WIDE:
        return np.ones(k)
    levels = np.array([10, -10, 5, -5, 0])
    if k % 512:
        return np.exp2(np.random.permutation(np.resize(levels, k // 32))).repeat(32)
    a = np.empty((k // 512, 16))
    for p in range(k // 512):
        a[p, :8] = np.random.permutation(np.resize(levels, 8))
        for g in range(8):
            far = levels[np.abs(levels - a[p, g]) >= 10]
            a[p, g + 8] = far[np.random.randint(len(far))]
    return np.exp2(a.ravel()).repeat(32)


def f64(x):
    return np.asarray(x).astype(np.float64)


def striped(idx):
    return np.tile(idx.reshape(-1, 16).T, (8, 1)).astype(np.uint16)


def unstriped(offs):
    return offs[:16].T.reshape(-1).astype(np.int64)


def pack_weight(w):
    k, n = w.shape
    w = f64(np.asarray(w, np.float32).astype(ml_dtypes.bfloat16)).reshape(k // 32, 32, n)
    amax = np.abs(w).max(1)
    byte = np.clip(np.where(amax > 0, np.frexp(amax)[1] - 1 + 127 - 7, 1), 1, 254)
    scaled = (w * np.exp2(127.0 - byte)[:, None, :]).reshape(k, n).astype(np.float32)
    words = np.ascontiguousarray(scaled.reshape(k // 512, 128, 4, n).transpose(0, 1, 3, 2)).astype(ml_dtypes.float8_e4m3fn).view(np.uint8)
    return words, np.ascontiguousarray(byte.astype(np.uint8).reshape(k // 512, 16, n))


def unpack_weight(words, scales):
    g, p, n, _ = words.shape
    vals = np.ascontiguousarray(words).view(ml_dtypes.float8_e4m3fn).astype(np.float64) * np.repeat(np.exp2(scales.astype(np.float64) - 127.0), 8, axis=1)[..., None]
    return vals.transpose(0, 1, 3, 2).reshape(g * 512, n)


K, T, E, C, N = 1024, 1024, 2, 256, 512


def by_expert(wq, xq):
    return np.concatenate([wq[e].T @ xq[:, e * C:(e + 1) * C] for e in range(E)], axis=1)


def setup_inputs():
    n = np.random.standard_normal
    s = mx_kscale(K)[:, None]
    packed = [pack_weight(m) for m in n((E, K, N)) / np.sqrt(K) / s[None]]
    return {
        "xT": (n((K, T)) * s).astype(np.float32),
        "w_words": np.stack([m[0] for m in packed]),
        "w_scales": np.stack([m[1] for m in packed]),
        "gate": np.tile(np.random.uniform(0.2, 1.0, E * C), (N, 1)).astype(np.float32),
        "offs": striped(np.random.permutation(T)[:E * C]),
    }


def reference(xT, w_words, w_scales, gate, offs):
    idx = unstriped(offs)
    xq = mxq(f64(xT)[:, idx], 0, "e4m3")
    w = np.stack([unpack_weight(w_words[e], w_scales[e]) for e in range(E)])
    y = by_expert(w, xq)
    out = np.zeros((N, T))
    out[:, idx] = f64(gate) * y
    return out

@@ -1,0 +1,131 @@
+from contextlib import ExitStack
+
+import concourse.mybir as mybir
+
+K, T, E, C, N = 1024, 1024, 2, 256, 512
+FLOPS = 2 * K * N * E * C
+
+F32 = mybir.dt.float32
+BF16 = mybir.dt.bfloat16
+U32 = mybir.dt.uint32
+I32 = mybir.dt.int32
+U16 = mybir.dt.uint16
+U8 = mybir.dt.uint8
+FP8X4 = mybir.dt.float8_e4m3fn_x4
+
+P = 128
+PACK = 4
+PASSES = K // (P * PACK)
+M_TILES = N // P
+LIST_COLS = C // 16
+
+
+def tile_routed_moe_kernel(tc, xT, w_words, w_scales, gate, offs, out):
+    nc = tc.nc
+    mult = mybir.AluOpType.mult
+
+    with ExitStack() as ctx:
+        lists = ctx.enter_context(tc.tile_pool(name="lists", bufs=1))
+        keep = ctx.enter_context(tc.tile_pool(name="keep", bufs=1))
+        psum = ctx.enter_context(tc.psum_pool(name="psum", bufs=1))
+
+        offsets = lists.tile([P, E * LIST_COLS], U16, name="offsets")
+        nc.sync.dma_start(offsets[:], offs)
+
+        plane = {}
+        gathered = {}
+        grouped = {}
+        x_codes = {}
+        x_scales = {}
+        for a in range(PASSES):
+            for t in range(PACK):
+                plane[a, t] = keep.tile([P, T], F32, name="plane%d%d" % (a, t))
+            for e in range(E):
+                gathered[a, e] = keep.tile([P, PACK, C], F32, name="gathered%d%d" % (a, e))
+                grouped[a, e] = keep.tile([P, C, PACK], BF16, name="grouped%d%d" % (a, e), align_bytes=64)
+                x_codes[a, e] = keep.tile([P, C], U32, name="xcodes%d%d" % (a, e), align_bytes=64)
+                x_scales[a, e] = keep.tile([P, C], U8, name="xscales%d%d" % (a, e), align_bytes=64)
+        w_planes = keep.tile([P, N], U8, name="w_planes", align_bytes=64)
+        w_codes = [keep.tile([P, E * PASSES, P], U32, name="wcodes%d" % m, align_bytes=64) for m in range(M_TILES)]
+        gate_sb = [keep.tile([P, E * C], F32, name="gate%d" % m) for m in range(M_TILES)]
+        window = [keep.tile([P, T], F32, name="window%d" % m) for m in range(M_TILES)]
+
+        nc.vector.memset(w_planes[:].bitcast(I32), 0)
+        for m in range(M_TILES):
+            nc.vector.memset(window[m][:], 0.0)
+
+        x_view = xT.rearrange("(a p t) n -> a p t n", p=P, t=PACK)
+        w_view = w_words.rearrange("e a p n r -> p (e a) (n r)")
+        s_view = w_scales.rearrange("e a q n -> (e a) q n")
+        for t in range(PACK):
+            nc.sync.dma_start(plane[0, t][:], x_view[0, :, t, :])
+        for q in range(4):
+            nc.sync.dma_start(
+                w_planes[32 * q : 32 * q + 16, :].bitcast(I32),
+                s_view[:, 4 * q : 4 * q + 4, :].bitcast(I32),
+            )
+        for t in range(PACK):
+            nc.sync.dma_start(plane[1, t][:], x_view[1, :, t, :])
+        for m in range(M_TILES):
+            nc.sync.dma_start(
+                w_codes[m][:].bitcast(I32),
+                w_view[:, :, 4 * P * m : 4 * P * (m + 1)].bitcast(I32),
+            )
+            nc.sync.dma_start(gate_sb[m][:], gate[P * m : P * (m + 1), :])
+
+        def gather(a, t, e):
+            nc.vector.tensor_copy(
+                gathered[a, e][:, t, :],
+                plane[a, t][:].indirect(offsets[:, LIST_COLS * e : LIST_COLS * (e + 1)]),
+            )
+
+        def interleave(engine_copy, a, e):
+            engine_copy(out=grouped[a, e][:], in_=gathered[a, e][:].rearrange("p t c -> p c t"))
+
+        def quantise(a, e):
+            nc.vector.quantize_mx(
+                out=x_codes[a, e][:].bitcast(FP8X4),
+                scales=x_scales[a, e][:],
+                in_=grouped[a, e][:].rearrange("p c t -> p (c t)"),
+            )
+
+        for t in range(PACK):
+            for e in range(E):
+                gather(0, t, e)
+        interleave(nc.scalar.copy, 0, 0)
+        interleave(nc.scalar.copy, 0, 1)
+        for t in range(PACK):
+            for e in range(E):
+                gather(1, t, e)
+            if t == 1:
+                quantise(0, 0)
+            if t == 2:
+                quantise(0, 1)
+        interleave(nc.scalar.copy, 1, 0)
+        interleave(nc.vector.tensor_copy, 1, 1)
+        quantise(1, 0)
+        quantise(1, 1)
+
+        for m in range(M_TILES):
+            for e in range(E):
+                acc = psum.tile([P, C], F32, name="acc%d%d" % (m, e))
+                for a in range(PASSES):
+                    j = e * PASSES + a
+                    nc.tensor.matmul_mx(
+                        out=acc[:],
+                        lhsT=w_codes[m][:, j, :].bitcast(FP8X4),
+                        lhsT_scale=w_planes[4 * j : P, P * m : P * (m + 1)],
+                        rhs=x_codes[a, e][:].bitcast(FP8X4),
+                        rhs_scale=x_scales[a, e][:],
+                        start=(a == 0),
+                        stop=(a == PASSES - 1),
+                    )
+                sums = keep.tile([P, C], F32, name="sums%d%d" % (m, e))
+                nc.scalar.copy(out=sums[:], in_=acc[:])
+                nc.vector.tensor_tensor(
+                    window[m][:].indirect(offsets[:, LIST_COLS * e : LIST_COLS * (e + 1)]),
+                    sums[:],
+                    gate_sb[m][:, C * e : C * (e + 1)],
+                    mult,
+                )
+            nc.sync.dma_start(out[P * m : P * (m + 1), :], window[m][:])

@@ -18,6 +18,7 @@ PACK = 4
 PASSES = K // (P * PACK)
 M_TILES = N // P
 LIST_COLS = C // 16
+LOAD_ORDER = ((0, 0), (0, 1), (1, 0), (0, 2), (1, 1), (0, 3), (1, 2), (1, 3))
 
 
 def tile_routed_moe_kernel(tc, xT, w_words, w_scales, gate, offs, out):
@@ -27,45 +28,48 @@ def tile_routed_moe_kernel(tc, xT, w_words, w_scales, gate, offs, out):
     with ExitStack() as ctx:
         lists = ctx.enter_context(tc.tile_pool(name="lists", bufs=1))
         keep = ctx.enter_context(tc.tile_pool(name="keep", bufs=1))
+        turn = ctx.enter_context(tc.tile_pool(name="turn", bufs=1))
         psum = ctx.enter_context(tc.psum_pool(name="psum", bufs=1))
 
         offsets = lists.tile([P, E * LIST_COLS], U16, name="offsets")
         nc.sync.dma_start(offsets[:], offs)
 
         plane = {}
-        gathered = {}
         grouped = {}
         x_codes = {}
         x_scales = {}
         for a in range(PASSES):
-            for t in range(PACK):
-                plane[a, t] = keep.tile([P, T], F32, name="plane%d%d" % (a, t))
             for e in range(E):
-                gathered[a, e] = keep.tile([P, PACK, C], F32, name="gathered%d%d" % (a, e))
-                grouped[a, e] = keep.tile([P, C, PACK], BF16, name="grouped%d%d" % (a, e), align_bytes=64)
                 x_codes[a, e] = keep.tile([P, C], U32, name="xcodes%d%d" % (a, e), align_bytes=64)
                 x_scales[a, e] = keep.tile([P, C], U8, name="xscales%d%d" % (a, e), align_bytes=64)
         w_planes = keep.tile([P, N], U8, name="w_planes", align_bytes=64)
         w_codes = [keep.tile([P, E * PASSES, P], U32, name="wcodes%d" % m, align_bytes=64) for m in range(M_TILES)]
         gate_sb = [keep.tile([P, E * C], F32, name="gate%d" % m) for m in range(M_TILES)]
         window = [keep.tile([P, T], F32, name="window%d" % m) for m in range(M_TILES)]
+        x_bf16 = keep.tile([P, PACK, T], BF16, name="x_bf16")
+        grouped[1, 0] = turn.tile([P, C, PACK], BF16, name="grouped10", tag="turn", align_bytes=64)
+        grouped[0, 0] = keep.tile([P, C, PACK], BF16, name="grouped00", align_bytes=64)
+        grouped[1, 1] = keep.tile([P, C, PACK], BF16, name="grouped11", align_bytes=64)
+        raw = [keep.tile([P, PACK, T], F32, name="raw%d" % a) for a in range(PASSES)]
+        for a in range(PASSES):
+            for t in range(PACK):
+                plane[a, t] = raw[a][:, t, :]
 
         nc.vector.memset(w_planes[:].bitcast(I32), 0)
         for m in range(M_TILES):
-            nc.vector.memset(window[m][:], 0.0)
+            (nc.vector if m < 2 else nc.gpsimd).memset(window[m][:], 0.0)
 
         x_view = xT.rearrange("(a p t) n -> a p t n", p=P, t=PACK)
         w_view = w_words.rearrange("e a p n r -> p (e a) (n r)")
         s_view = w_scales.rearrange("e a q n -> (e a) q n")
-        for t in range(PACK):
-            nc.sync.dma_start(plane[0, t][:], x_view[0, :, t, :])
-        for q in range(4):
-            nc.sync.dma_start(
-                w_planes[32 * q : 32 * q + 16, :].bitcast(I32),
-                s_view[:, 4 * q : 4 * q + 4, :].bitcast(I32),
-            )
-        for t in range(PACK):
-            nc.sync.dma_start(plane[1, t][:], x_view[1, :, t, :])
+        for i, (a, t) in enumerate(LOAD_ORDER):
+            nc.sync.dma_start(plane[a, t], x_view[a, :, t, :])
+            if i == 3:
+                for q in range(4):
+                    nc.sync.dma_start(
+                        w_planes[32 * q : 32 * q + 16, :].bitcast(I32),
+                        s_view[:, 4 * q : 4 * q + 4, :].bitcast(I32),
+                    )
         for m in range(M_TILES):
             nc.sync.dma_start(
                 w_codes[m][:].bitcast(I32),
@@ -75,12 +79,9 @@ def tile_routed_moe_kernel(tc, xT, w_words, w_scales, gate, offs, out):
 
         def gather(a, t, e):
             nc.vector.tensor_copy(
-                gathered[a, e][:, t, :],
-                plane[a, t][:].indirect(offsets[:, LIST_COLS * e : LIST_COLS * (e + 1)]),
+                grouped[a, e][:, :, t],
+                plane[a, t].indirect(offsets[:, LIST_COLS * e : LIST_COLS * (e + 1)]),
             )
-
-        def interleave(engine_copy, a, e):
-            engine_copy(out=grouped[a, e][:], in_=gathered[a, e][:].rearrange("p t c -> p c t"))
 
         def quantise(a, e):
             nc.vector.quantize_mx(
@@ -89,25 +90,24 @@ def tile_routed_moe_kernel(tc, xT, w_words, w_scales, gate, offs, out):
                 in_=grouped[a, e][:].rearrange("p c t -> p (c t)"),
             )
 
-        for t in range(PACK):
-            for e in range(E):
-                gather(0, t, e)
-        interleave(nc.scalar.copy, 0, 0)
-        interleave(nc.scalar.copy, 0, 1)
-        for t in range(PACK):
-            for e in range(E):
-                gather(1, t, e)
-            if t == 1:
-                quantise(0, 0)
-            if t == 2:
-                quantise(0, 1)
-        interleave(nc.scalar.copy, 1, 0)
-        interleave(nc.vector.tensor_copy, 1, 1)
-        quantise(1, 0)
-        quantise(1, 1)
+        def scalar_gather(t, e):
+            nc.scalar.activation(
+                grouped[0, e][:, :, t],
+                x_bf16[:, t, :].indirect(offsets[:, LIST_COLS * e : LIST_COLS * (e + 1)]),
+                mybir.ActivationFunctionType.Copy,
+            )
 
-        for m in range(M_TILES):
-            for e in range(E):
+        for e in range(E):
+            if e == 1:
+                grouped[0, 1] = turn.tile([P, C, PACK], BF16, name="grouped01", tag="turn", align_bytes=64)
+            for t in range(PACK):
+                if e == 0:
+                    (nc.vector.tensor_copy if t < 2 else nc.scalar.copy)(out=x_bf16[:, t, :], in_=plane[0, t])
+                scalar_gather(t, e)
+                gather(1, t, e)
+            quantise(0, e)
+            quantise(1, e)
+            for m in range(M_TILES):
                 acc = psum.tile([P, C], F32, name="acc%d%d" % (m, e))
                 for a in range(PASSES):
                     j = e * PASSES + a
@@ -128,4 +128,5 @@ def tile_routed_moe_kernel(tc, xT, w_words, w_scales, gate, offs, out):
                     gate_sb[m][:, C * e : C * (e + 1)],
                     mult,
                 )
-            nc.sync.dma_start(out[P * m : P * (m + 1), :], window[m][:])
+                if e == E - 1:
+                    nc.sync.dma_start(out[P * m : P * (m + 1), :], window[m][:])

@@ -107,6 +107,16 @@ def tile_routed_moe_kernel(tc, xT, w_words, w_scales, gate, offs, out):
                 gather(1, t, e)
             quantise(0, e)
             quantise(1, e)
+            sums = {}
+
+            def scatter(m):
+                nc.vector.tensor_copy(
+                    window[m][:].indirect(offsets[:, LIST_COLS * e : LIST_COLS * (e + 1)]),
+                    sums[m][:],
+                )
+                if e == E - 1:
+                    nc.sync.dma_start(out[P * m : P * (m + 1), :], window[m][:])
+
             for m in range(M_TILES):
                 acc = psum.tile([P, C], F32, name="acc%d%d" % (m, e))
                 for a in range(PASSES):
@@ -120,13 +130,8 @@ def tile_routed_moe_kernel(tc, xT, w_words, w_scales, gate, offs, out):
                         start=(a == 0),
                         stop=(a == PASSES - 1),
                     )
-                sums = keep.tile([P, C], F32, name="sums%d%d" % (m, e))
-                nc.scalar.copy(out=sums[:], in_=acc[:])
-                nc.vector.tensor_tensor(
-                    window[m][:].indirect(offsets[:, LIST_COLS * e : LIST_COLS * (e + 1)]),
-                    sums[:],
-                    gate_sb[m][:, C * e : C * (e + 1)],
-                    mult,
-                )
-                if e == E - 1:
-                    nc.sync.dma_start(out[P * m : P * (m + 1), :], window[m][:])
+                sums[m] = keep.tile([P, C], F32, name="sums%d%d" % (m, e))
+                nc.vector.tensor_tensor(sums[m][:], acc[:], gate_sb[m][:, C * e : C * (e + 1)], mult)
+                if m > 0:
+                    scatter(m - 1)
+            scatter(M_TILES - 1)

@@ -28,32 +28,29 @@ def tile_routed_moe_kernel(tc, xT, w_words, w_scales, gate, offs, out):
     with ExitStack() as ctx:
         lists = ctx.enter_context(tc.tile_pool(name="lists", bufs=1))
         keep = ctx.enter_context(tc.tile_pool(name="keep", bufs=1))
-        turn = ctx.enter_context(tc.tile_pool(name="turn", bufs=1))
         psum = ctx.enter_context(tc.psum_pool(name="psum", bufs=1))
 
         offsets = lists.tile([P, E * LIST_COLS], U16, name="offsets")
         nc.sync.dma_start(offsets[:], offs)
 
-        plane = {}
+        def expert_list(e):
+            return offsets[:, LIST_COLS * e : LIST_COLS * (e + 1)]
+
+        pair = [keep.tile([P, 2 * T], F32, name="pair%d" % t) for t in range(PACK)]
+        x_bf16 = keep.tile([P, PACK, T], BF16, name="x_bf16")
+        gathered = keep.tile([P, PACK, E * C], F32, name="gathered")
         grouped = {}
         x_codes = {}
         x_scales = {}
         for a in range(PASSES):
             for e in range(E):
+                grouped[a, e] = keep.tile([P, C, PACK], BF16, name="grouped%d%d" % (a, e), align_bytes=64)
                 x_codes[a, e] = keep.tile([P, C], U32, name="xcodes%d%d" % (a, e), align_bytes=64)
                 x_scales[a, e] = keep.tile([P, C], U8, name="xscales%d%d" % (a, e), align_bytes=64)
         w_planes = keep.tile([P, N], U8, name="w_planes", align_bytes=64)
         w_codes = [keep.tile([P, E * PASSES, P], U32, name="wcodes%d" % m, align_bytes=64) for m in range(M_TILES)]
         gate_sb = [keep.tile([P, E * C], F32, name="gate%d" % m) for m in range(M_TILES)]
         window = [keep.tile([P, T], F32, name="window%d" % m) for m in range(M_TILES)]
-        x_bf16 = keep.tile([P, PACK, T], BF16, name="x_bf16")
-        grouped[1, 0] = turn.tile([P, C, PACK], BF16, name="grouped10", tag="turn", align_bytes=64)
-        grouped[0, 0] = keep.tile([P, C, PACK], BF16, name="grouped00", align_bytes=64)
-        grouped[1, 1] = keep.tile([P, C, PACK], BF16, name="grouped11", align_bytes=64)
-        raw = [keep.tile([P, PACK, T], F32, name="raw%d" % a) for a in range(PASSES)]
-        for a in range(PASSES):
-            for t in range(PACK):
-                plane[a, t] = raw[a][:, t, :]
 
         nc.vector.memset(w_planes[:].bitcast(I32), 0)
         for m in range(M_TILES):
@@ -63,7 +60,7 @@ def tile_routed_moe_kernel(tc, xT, w_words, w_scales, gate, offs, out):
         w_view = w_words.rearrange("e a p n r -> p (e a) (n r)")
         s_view = w_scales.rearrange("e a q n -> (e a) q n")
         for i, (a, t) in enumerate(LOAD_ORDER):
-            nc.sync.dma_start(plane[a, t], x_view[a, :, t, :])
+            nc.sync.dma_start(pair[t][:, T * (1 - a) : T * (2 - a)], x_view[a, :, t, :])
             if i == 3:
                 for q in range(4):
                     nc.sync.dma_start(
@@ -77,12 +74,6 @@ def tile_routed_moe_kernel(tc, xT, w_words, w_scales, gate, offs, out):
             )
             nc.sync.dma_start(gate_sb[m][:], gate[P * m : P * (m + 1), :])
 
-        def gather(a, t, e):
-            nc.vector.tensor_copy(
-                grouped[a, e][:, :, t],
-                plane[a, t].indirect(offsets[:, LIST_COLS * e : LIST_COLS * (e + 1)]),
-            )
-
         def quantise(a, e):
             nc.vector.quantize_mx(
                 out=x_codes[a, e][:].bitcast(FP8X4),
@@ -90,33 +81,29 @@ def tile_routed_moe_kernel(tc, xT, w_words, w_scales, gate, offs, out):
                 in_=grouped[a, e][:].rearrange("p c t -> p (c t)"),
             )
 
-        def scalar_gather(t, e):
-            nc.scalar.activation(
-                grouped[0, e][:, :, t],
-                x_bf16[:, t, :].indirect(offsets[:, LIST_COLS * e : LIST_COLS * (e + 1)]),
-                mybir.ActivationFunctionType.Copy,
+        def interleave(engine_copy, e):
+            engine_copy(
+                out=grouped[1, e][:],
+                in_=gathered[:, :, C * e : C * (e + 1)].rearrange("p t c -> p c t"),
             )
 
+        for t in range(PACK):
+            nc.vector.tensor_copy(out=x_bf16[:, t, :], in_=pair[t][:, T : 2 * T])
+            for e in range(E):
+                nc.scalar.activation(
+                    grouped[0, e][:, :, t],
+                    x_bf16[:, t, :].indirect(expert_list(e)),
+                    mybir.ActivationFunctionType.Copy,
+                )
+            if t < PACK - 1:
+                nc.vector.tensor_copy(gathered[:, t, :], pair[t][:].indirect(offsets[:]))
+
+        last = PACK - 1
         for e in range(E):
-            if e == 1:
-                grouped[0, 1] = turn.tile([P, C, PACK], BF16, name="grouped01", tag="turn", align_bytes=64)
-            for t in range(PACK):
-                if e == 0:
-                    (nc.vector.tensor_copy if t < 2 else nc.scalar.copy)(out=x_bf16[:, t, :], in_=plane[0, t])
-                scalar_gather(t, e)
-                gather(1, t, e)
+            nc.vector.tensor_copy(gathered[:, last, C * e : C * (e + 1)], pair[last][:].indirect(expert_list(e)))
+            interleave(nc.vector.tensor_copy if e == 0 else nc.scalar.copy, e)
             quantise(0, e)
             quantise(1, e)
-            sums = {}
-
-            def scatter(m):
-                nc.vector.tensor_copy(
-                    window[m][:].indirect(offsets[:, LIST_COLS * e : LIST_COLS * (e + 1)]),
-                    sums[m][:],
-                )
-                if e == E - 1:
-                    nc.sync.dma_start(out[P * m : P * (m + 1), :], window[m][:])
-
             for m in range(M_TILES):
                 acc = psum.tile([P, C], F32, name="acc%d%d" % (m, e))
                 for a in range(PASSES):
@@ -130,8 +117,13 @@ def tile_routed_moe_kernel(tc, xT, w_words, w_scales, gate, offs, out):
                         start=(a == 0),
                         stop=(a == PASSES - 1),
                     )
-                sums[m] = keep.tile([P, C], F32, name="sums%d%d" % (m, e))
-                nc.vector.tensor_tensor(sums[m][:], acc[:], gate_sb[m][:, C * e : C * (e + 1)], mult)
-                if m > 0:
-                    scatter(m - 1)
-            scatter(M_TILES - 1)
+                sums = keep.tile([P, C], F32, name="sums%d%d" % (m, e))
+                nc.scalar.copy(out=sums[:], in_=acc[:])
+                nc.vector.tensor_tensor(
+                    window[m][:].indirect(expert_list(e)),
+                    sums[:],
+                    gate_sb[m][:, C * e : C * (e + 1)],
+                    mult,
+                )
+                if e == E - 1:
+                    nc.sync.dma_start(out[P * m : P * (m + 1), :], window[m][:])

@@ -18,16 +18,21 @@ PACK = 4
 PASSES = K // (P * PACK)
 M_TILES = N // P
 LIST_COLS = C // 16
+SPLIT_BLOCKS = 2
+LAST_PLANE = (1, 3)
+BACK_ORDER = tuple(range(SPLIT_BLOCKS, M_TILES)) + tuple(range(SPLIT_BLOCKS))
 LOAD_ORDER = ((0, 0), (0, 1), (1, 0), (0, 2), (1, 1), (0, 3), (1, 2), (1, 3))
 
 
 def tile_routed_moe_kernel(tc, xT, w_words, w_scales, gate, offs, out):
     nc = tc.nc
     mult = mybir.AluOpType.mult
+    copy_fn = mybir.ActivationFunctionType.Copy
 
     with ExitStack() as ctx:
         lists = ctx.enter_context(tc.tile_pool(name="lists", bufs=1))
         keep = ctx.enter_context(tc.tile_pool(name="keep", bufs=1))
+        turn = ctx.enter_context(tc.tile_pool(name="turn", bufs=1))
         psum = ctx.enter_context(tc.psum_pool(name="psum", bufs=1))
 
         offsets = lists.tile([P, E * LIST_COLS], U16, name="offsets")
@@ -36,94 +41,109 @@ def tile_routed_moe_kernel(tc, xT, w_words, w_scales, gate, offs, out):
         def expert_list(e):
             return offsets[:, LIST_COLS * e : LIST_COLS * (e + 1)]
 
-        pair = [keep.tile([P, 2 * T], F32, name="pair%d" % t) for t in range(PACK)]
+        def slots(e):
+            return slice(C * e, C * (e + 1))
+
+        plane = {}
+        for a in range(PASSES):
+            for t in range(PACK):
+                if (a, t) != LAST_PLANE:
+                    plane[a, t] = keep.tile([P, T], F32, name="plane%d%d" % (a, t))
+        plane[LAST_PLANE] = turn.tile([P, T], F32, name="last_plane", tag="turn", align_bytes=64)
         x_bf16 = keep.tile([P, PACK, T], BF16, name="x_bf16")
-        gathered = keep.tile([P, PACK, E * C], F32, name="gathered")
-        grouped = {}
+        grouped = [keep.tile([P, E * C, PACK], BF16, name="grouped%d" % a, align_bytes=64) for a in range(PASSES)]
         x_codes = {}
         x_scales = {}
         for a in range(PASSES):
             for e in range(E):
-                grouped[a, e] = keep.tile([P, C, PACK], BF16, name="grouped%d%d" % (a, e), align_bytes=64)
-                x_codes[a, e] = keep.tile([P, C], U32, name="xcodes%d%d" % (a, e), align_bytes=64)
+                if (a, e) != (0, 1):
+                    x_codes[a, e] = keep.tile([P, C], U32, name="xcodes%d%d" % (a, e), align_bytes=64)
                 x_scales[a, e] = keep.tile([P, C], U8, name="xscales%d%d" % (a, e), align_bytes=64)
         w_planes = keep.tile([P, N], U8, name="w_planes", align_bytes=64)
-        w_codes = [keep.tile([P, E * PASSES, P], U32, name="wcodes%d" % m, align_bytes=64) for m in range(M_TILES)]
+        w_codes = [keep.tile([P, N], U32, name="wcodes%d" % j, align_bytes=64) for j in range(E * PASSES)]
         gate_sb = [keep.tile([P, E * C], F32, name="gate%d" % m) for m in range(M_TILES)]
         window = [keep.tile([P, T], F32, name="window%d" % m) for m in range(M_TILES)]
+        sums = [keep.tile([P, E * C], F32, name="sums%d" % m) for m in range(M_TILES)]
 
         nc.vector.memset(w_planes[:].bitcast(I32), 0)
         for m in range(M_TILES):
             (nc.vector if m < 2 else nc.gpsimd).memset(window[m][:], 0.0)
 
         x_view = xT.rearrange("(a p t) n -> a p t n", p=P, t=PACK)
-        w_view = w_words.rearrange("e a p n r -> p (e a) (n r)")
+        w_view = w_words.rearrange("e a p n r -> (e a) p (n r)")
         s_view = w_scales.rearrange("e a q n -> (e a) q n")
-        for i, (a, t) in enumerate(LOAD_ORDER):
-            nc.sync.dma_start(pair[t][:, T * (1 - a) : T * (2 - a)], x_view[a, :, t, :])
-            if i == 3:
-                for q in range(4):
-                    nc.sync.dma_start(
-                        w_planes[32 * q : 32 * q + 16, :].bitcast(I32),
-                        s_view[:, 4 * q : 4 * q + 4, :].bitcast(I32),
-                    )
-        for m in range(M_TILES):
-            nc.sync.dma_start(
-                w_codes[m][:].bitcast(I32),
-                w_view[:, :, 4 * P * m : 4 * P * (m + 1)].bitcast(I32),
-            )
+
+        def load_scales():
+            for q in range(4):
+                nc.sync.dma_start(
+                    w_planes[32 * q : 32 * q + 16, :].bitcast(I32),
+                    s_view[:, 4 * q : 4 * q + 4, :].bitcast(I32),
+                )
+
+        def load_weights(e):
+            for a in range(PASSES):
+                j = e * PASSES + a
+                nc.sync.dma_start(w_codes[j][:].bitcast(I32), w_view[j].bitcast(I32))
+
+        def load_gate(m):
             nc.sync.dma_start(gate_sb[m][:], gate[P * m : P * (m + 1), :])
+
+        for i, (a, t) in enumerate(LOAD_ORDER):
+            nc.sync.dma_start(plane[a, t][:], x_view[a, :, t, :])
+            if i == 3:
+                load_scales()
+        load_weights(0)
+        load_gate(0)
+        load_gate(1)
+        load_weights(1)
+        load_gate(2)
+        load_gate(3)
 
         def quantise(a, e):
             nc.vector.quantize_mx(
                 out=x_codes[a, e][:].bitcast(FP8X4),
                 scales=x_scales[a, e][:],
-                in_=grouped[a, e][:].rearrange("p c t -> p (c t)"),
-            )
-
-        def interleave(engine_copy, e):
-            engine_copy(
-                out=grouped[1, e][:],
-                in_=gathered[:, :, C * e : C * (e + 1)].rearrange("p t c -> p c t"),
+                in_=grouped[a][:, slots(e), :].rearrange("p c t -> p (c t)"),
             )
 
         for t in range(PACK):
-            nc.vector.tensor_copy(out=x_bf16[:, t, :], in_=pair[t][:, T : 2 * T])
+            nc.vector.tensor_copy(out=x_bf16[:, t, :], in_=plane[0, t][:])
             for e in range(E):
-                nc.scalar.activation(
-                    grouped[0, e][:, :, t],
-                    x_bf16[:, t, :].indirect(expert_list(e)),
-                    mybir.ActivationFunctionType.Copy,
-                )
-            if t < PACK - 1:
-                nc.vector.tensor_copy(gathered[:, t, :], pair[t][:].indirect(offsets[:]))
+                nc.scalar.activation(grouped[0][:, slots(e), t], x_bf16[:, t, :].indirect(expert_list(e)), copy_fn)
+            nc.vector.tensor_copy(grouped[1][:, :, t], plane[1, t][:].indirect(offsets[:]))
 
-        last = PACK - 1
+        x_codes[0, 1] = turn.tile([P, C], U32, name="xcodes01", tag="turn", align_bytes=64)
         for e in range(E):
-            nc.vector.tensor_copy(gathered[:, last, C * e : C * (e + 1)], pair[last][:].indirect(expert_list(e)))
-            interleave(nc.vector.tensor_copy if e == 0 else nc.scalar.copy, e)
             quantise(0, e)
             quantise(1, e)
-            for m in range(M_TILES):
+            for m in (range(M_TILES) if e == 0 else BACK_ORDER):
                 acc = psum.tile([P, C], F32, name="acc%d%d" % (m, e))
                 for a in range(PASSES):
                     j = e * PASSES + a
                     nc.tensor.matmul_mx(
                         out=acc[:],
-                        lhsT=w_codes[m][:, j, :].bitcast(FP8X4),
+                        lhsT=w_codes[j][:, P * m : P * (m + 1)].bitcast(FP8X4),
                         lhsT_scale=w_planes[4 * j : P, P * m : P * (m + 1)],
                         rhs=x_codes[a, e][:].bitcast(FP8X4),
                         rhs_scale=x_scales[a, e][:],
                         start=(a == 0),
                         stop=(a == PASSES - 1),
                     )
-                sums = keep.tile([P, C], F32, name="sums%d%d" % (m, e))
-                nc.scalar.copy(out=sums[:], in_=acc[:])
-                nc.vector.tensor_tensor(
-                    window[m][:].indirect(expert_list(e)),
-                    sums[:],
-                    gate_sb[m][:, C * e : C * (e + 1)],
-                    mult,
-                )
-                if e == E - 1:
-                    nc.sync.dma_start(out[P * m : P * (m + 1), :], window[m][:])
+                nc.scalar.copy(out=sums[m][:, slots(e)], in_=acc[:])
+
+        def scatter_half(m, e):
+            nc.vector.tensor_tensor(
+                window[m][:].indirect(expert_list(e)), sums[m][:, slots(e)], gate_sb[m][:, slots(e)], mult
+            )
+
+        def store(m):
+            nc.sync.dma_start(out[P * m : P * (m + 1), :], window[m][:])
+
+        for m in range(SPLIT_BLOCKS):
+            scatter_half(m, 0)
+        for m in range(SPLIT_BLOCKS, M_TILES):
+            nc.vector.tensor_tensor(window[m][:].indirect(offsets[:]), sums[m][:], gate_sb[m][:], mult)
+            store(m)
+        for m in range(SPLIT_BLOCKS):
+            scatter_half(m, 1)
+            store(m)

@@ -90,7 +90,7 @@ def tile_routed_moe_kernel(tc, xT, w_words, w_scales, gate, offs, out):
 
         for i, (a, t) in enumerate(LOAD_ORDER):
             nc.sync.dma_start(plane[a, t][:], x_view[a, :, t, :])
-            if i == 3:
+            if i == 7:
                 load_scales()
         load_weights(0)
         load_gate(0)

@@ -19,7 +19,6 @@ PASSES = K // (P * PACK)
 M_TILES = N // P
 LIST_COLS = C // 16
 SPLIT_BLOCKS = 2
-LAST_PLANE = (1, 3)
 BACK_ORDER = tuple(range(SPLIT_BLOCKS, M_TILES)) + tuple(range(SPLIT_BLOCKS))
 LOAD_ORDER = ((0, 0), (0, 1), (1, 0), (0, 2), (1, 1), (0, 3), (1, 2), (1, 3))
 
@@ -47,11 +46,13 @@ def tile_routed_moe_kernel(tc, xT, w_words, w_scales, gate, offs, out):
         plane = {}
         for a in range(PASSES):
             for t in range(PACK):
-                if (a, t) != LAST_PLANE:
-                    plane[a, t] = keep.tile([P, T], F32, name="plane%d%d" % (a, t))
-        plane[LAST_PLANE] = turn.tile([P, T], F32, name="last_plane", tag="turn", align_bytes=64)
+                plane[a, t] = keep.tile([P, T], F32, name="plane%d%d" % (a, t))
         x_bf16 = keep.tile([P, PACK, T], BF16, name="x_bf16")
-        grouped = [keep.tile([P, E * C, PACK], BF16, name="grouped%d" % a, align_bytes=64) for a in range(PASSES)]
+        gathered = turn.tile([P, PACK, E * C], F32, name="gathered", tag="turn", align_bytes=64)
+        grouped = {}
+        for a in range(PASSES):
+            for e in range(E):
+                grouped[a, e] = keep.tile([P, C, PACK], BF16, name="grouped%d%d" % (a, e), align_bytes=64)
         x_codes = {}
         x_scales = {}
         for a in range(PASSES):
@@ -103,14 +104,16 @@ def tile_routed_moe_kernel(tc, xT, w_words, w_scales, gate, offs, out):
             nc.vector.quantize_mx(
                 out=x_codes[a, e][:].bitcast(FP8X4),
                 scales=x_scales[a, e][:],
-                in_=grouped[a][:, slots(e), :].rearrange("p c t -> p (c t)"),
+                in_=grouped[a, e][:].rearrange("p c t -> p (c t)"),
             )
 
         for t in range(PACK):
             nc.vector.tensor_copy(out=x_bf16[:, t, :], in_=plane[0, t][:])
             for e in range(E):
-                nc.scalar.activation(grouped[0][:, slots(e), t], x_bf16[:, t, :].indirect(expert_list(e)), copy_fn)
-            nc.vector.tensor_copy(grouped[1][:, :, t], plane[1, t][:].indirect(offsets[:]))
+                nc.scalar.activation(grouped[0, e][:, :, t], x_bf16[:, t, :].indirect(expert_list(e)), copy_fn)
+            nc.vector.tensor_copy(gathered[:, t, :], plane[1, t][:].indirect(offsets[:]))
+        nc.vector.tensor_copy(out=grouped[1, 0][:], in_=gathered[:, :, slots(0)].rearrange("p t c -> p c t"))
+        nc.scalar.copy(out=grouped[1, 1][:], in_=gathered[:, :, slots(1)].rearrange("p t c -> p c t"))
 
         x_codes[0, 1] = turn.tile([P, C], U32, name="xcodes01", tag="turn", align_bytes=64)
         for e in range(E):

@@ -48,11 +48,8 @@ def tile_routed_moe_kernel(tc, xT, w_words, w_scales, gate, offs, out):
             for t in range(PACK):
                 plane[a, t] = keep.tile([P, T], F32, name="plane%d%d" % (a, t))
         x_bf16 = keep.tile([P, PACK, T], BF16, name="x_bf16")
-        gathered = turn.tile([P, PACK, E * C], F32, name="gathered", tag="turn", align_bytes=64)
-        grouped = {}
-        for a in range(PASSES):
-            for e in range(E):
-                grouped[a, e] = keep.tile([P, C, PACK], BF16, name="grouped%d%d" % (a, e), align_bytes=64)
+        late_pair = turn.tile([P, 2, E * C], F32, name="late_pair", tag="turn", align_bytes=64)
+        grouped = [keep.tile([P, E * C, PACK], BF16, name="grouped%d" % a, align_bytes=64) for a in range(PASSES)]
         x_codes = {}
         x_scales = {}
         for a in range(PASSES):
@@ -104,16 +101,22 @@ def tile_routed_moe_kernel(tc, xT, w_words, w_scales, gate, offs, out):
             nc.vector.quantize_mx(
                 out=x_codes[a, e][:].bitcast(FP8X4),
                 scales=x_scales[a, e][:],
-                in_=grouped[a, e][:].rearrange("p c t -> p (c t)"),
+                in_=grouped[a][:, slots(e), :].rearrange("p c t -> p (c t)"),
             )
+
+        def interleave(engine_copy, pair, t0, cols):
+            engine_copy(out=grouped[1][:, cols, t0 : t0 + 2], in_=pair[:, :, cols].rearrange("p t c -> p c t"))
 
         for t in range(PACK):
             nc.vector.tensor_copy(out=x_bf16[:, t, :], in_=plane[0, t][:])
             for e in range(E):
-                nc.scalar.activation(grouped[0, e][:, :, t], x_bf16[:, t, :].indirect(expert_list(e)), copy_fn)
-            nc.vector.tensor_copy(gathered[:, t, :], plane[1, t][:].indirect(offsets[:]))
-        nc.vector.tensor_copy(out=grouped[1, 0][:], in_=gathered[:, :, slots(0)].rearrange("p t c -> p c t"))
-        nc.scalar.copy(out=grouped[1, 1][:], in_=gathered[:, :, slots(1)].rearrange("p t c -> p c t"))
+                nc.scalar.activation(grouped[0][:, slots(e), t], x_bf16[:, t, :].indirect(expert_list(e)), copy_fn)
+            if t < 2:
+                nc.vector.tensor_copy(grouped[1][:, :, t], plane[1, t][:].indirect(offsets[:]))
+            else:
+                nc.vector.tensor_copy(late_pair[:, t - 2, :], plane[1, t][:].indirect(offsets[:]))
+        interleave(nc.vector.tensor_copy, late_pair, 2, slots(0))
+        interleave(nc.scalar.copy, late_pair, 2, slots(1))
 
         x_codes[0, 1] = turn.tile([P, C], U32, name="xcodes01", tag="turn", align_bytes=64)
         for e in range(E):

@@ -20,7 +20,7 @@ M_TILES = N // P
 LIST_COLS = C // 16
 SPLIT_BLOCKS = 2
 BACK_ORDER = tuple(range(SPLIT_BLOCKS, M_TILES)) + tuple(range(SPLIT_BLOCKS))
-LOAD_ORDER = ((0, 0), (0, 1), (1, 0), (0, 2), (1, 1), (0, 3), (1, 2), (1, 3))
+LOAD_ORDER = ((0, 0), (0, 2), (0, 1), (0, 3), (1, 0), (1, 2), (1, 1), (1, 3))
 
 
 def tile_routed_moe_kernel(tc, xT, w_words, w_scales, gate, offs, out):
@@ -31,7 +31,6 @@ def tile_routed_moe_kernel(tc, xT, w_words, w_scales, gate, offs, out):
     with ExitStack() as ctx:
         lists = ctx.enter_context(tc.tile_pool(name="lists", bufs=1))
         keep = ctx.enter_context(tc.tile_pool(name="keep", bufs=1))
-        turn = ctx.enter_context(tc.tile_pool(name="turn", bufs=1))
         psum = ctx.enter_context(tc.psum_pool(name="psum", bufs=1))
 
         offsets = lists.tile([P, E * LIST_COLS], U16, name="offsets")
@@ -48,14 +47,12 @@ def tile_routed_moe_kernel(tc, xT, w_words, w_scales, gate, offs, out):
             for t in range(PACK):
                 plane[a, t] = keep.tile([P, T], F32, name="plane%d%d" % (a, t))
         x_bf16 = keep.tile([P, PACK, T], BF16, name="x_bf16")
-        late_pair = turn.tile([P, 2, E * C], F32, name="late_pair", tag="turn", align_bytes=64)
         grouped = [keep.tile([P, E * C, PACK], BF16, name="grouped%d" % a, align_bytes=64) for a in range(PASSES)]
         x_codes = {}
         x_scales = {}
         for a in range(PASSES):
             for e in range(E):
-                if (a, e) != (0, 1):
-                    x_codes[a, e] = keep.tile([P, C], U32, name="xcodes%d%d" % (a, e), align_bytes=64)
+                x_codes[a, e] = keep.tile([P, C], U32, name="xcodes%d%d" % (a, e), align_bytes=64)
                 x_scales[a, e] = keep.tile([P, C], U8, name="xscales%d%d" % (a, e), align_bytes=64)
         w_planes = keep.tile([P, N], U8, name="w_planes", align_bytes=64)
         w_codes = [keep.tile([P, N], U32, name="wcodes%d" % j, align_bytes=64) for j in range(E * PASSES)]
@@ -104,24 +101,22 @@ def tile_routed_moe_kernel(tc, xT, w_words, w_scales, gate, offs, out):
                 in_=grouped[a][:, slots(e), :].rearrange("p c t -> p (c t)"),
             )
 
-        def interleave(engine_copy, pair, t0, cols):
-            engine_copy(out=grouped[1][:, cols, t0 : t0 + 2], in_=pair[:, :, cols].rearrange("p t c -> p c t"))
-
-        for t in range(PACK):
-            nc.vector.tensor_copy(out=x_bf16[:, t, :], in_=plane[0, t][:])
-            for e in range(E):
-                nc.scalar.activation(grouped[0][:, slots(e), t], x_bf16[:, t, :].indirect(expert_list(e)), copy_fn)
+        for a, t in LOAD_ORDER:
             if t < 2:
-                nc.vector.tensor_copy(grouped[1][:, :, t], plane[1, t][:].indirect(offsets[:]))
-            else:
-                nc.vector.tensor_copy(late_pair[:, t - 2, :], plane[1, t][:].indirect(offsets[:]))
-        interleave(nc.vector.tensor_copy, late_pair, 2, slots(0))
-        interleave(nc.scalar.copy, late_pair, 2, slots(1))
-
-        x_codes[0, 1] = turn.tile([P, C], U32, name="xcodes01", tag="turn", align_bytes=64)
+                (nc.scalar.copy if (a, t) == (1, 0) else nc.vector.tensor_copy)(out=x_bf16[:, 2 * a + t, :], in_=plane[a, t][:])
+                for e in range(E):
+                    nc.scalar.activation(grouped[a][:, slots(e), t], x_bf16[:, 2 * a + t, :].indirect(expert_list(e)), copy_fn)
+            elif (a, t) != LOAD_ORDER[-1]:
+                nc.vector.tensor_copy(grouped[a][:, :, t], plane[a, t][:].indirect(offsets[:]))
+            if (a, t) == (0, 3):
+                quantise(0, 0)
+                quantise(0, 1)
+        a, t = LOAD_ORDER[-1]
         for e in range(E):
-            quantise(0, e)
+            nc.vector.tensor_copy(grouped[a][:, slots(e), t], plane[a, t][:].indirect(expert_list(e)))
             quantise(1, e)
+
+        for e in range(E):
             for m in (range(M_TILES) if e == 0 else BACK_ORDER):
                 acc = psum.tile([P, C], F32, name="acc%d%d" % (m, e))
                 for a in range(PASSES):

@@ -75,10 +75,12 @@ def tile_routed_moe_kernel(tc, xT, w_words, w_scales, gate, offs, out):
                     s_view[:, 4 * q : 4 * q + 4, :].bitcast(I32),
                 )
 
-        def load_weights(e):
+        def load_weights(e, first, last):
             for a in range(PASSES):
                 j = e * PASSES + a
-                nc.sync.dma_start(w_codes[j][:].bitcast(I32), w_view[j].bitcast(I32))
+                nc.sync.dma_start(
+                    w_codes[j][:, P * first : P * last].bitcast(I32), w_view[j][:, PACK * P * first : PACK * P * last].bitcast(I32)
+                )
 
         def load_gate(m):
             nc.sync.dma_start(gate_sb[m][:], gate[P * m : P * (m + 1), :])
@@ -87,10 +89,11 @@ def tile_routed_moe_kernel(tc, xT, w_words, w_scales, gate, offs, out):
             nc.sync.dma_start(plane[a, t][:], x_view[a, :, t, :])
             if i == 7:
                 load_scales()
-        load_weights(0)
+        load_weights(0, 0, 2)
         load_gate(0)
+        load_weights(0, 2, M_TILES)
         load_gate(1)
-        load_weights(1)
+        load_weights(1, 0, M_TILES)
         load_gate(2)
         load_gate(3)
 

@@ -60,6 +60,11 @@ def tile_routed_moe_kernel(tc, xT, w_words, w_scales, gate, offs, out):
         window = [keep.tile([P, T], F32, name="window%d" % m) for m in range(M_TILES)]
         sums = [keep.tile([P, E * C], F32, name="sums%d" % m) for m in range(M_TILES)]
 
+        warm_in = keep.tile([P, 1], F32, name="warm_in")
+        warm_out = keep.tile([P, 1], F32, name="warm_out")
+        nc.gpsimd.memset(warm_in[:], 0.0)
+        nc.scalar.activation(warm_out[:], warm_in[:], copy_fn)
+
         nc.vector.memset(w_planes[:].bitcast(I32), 0)
         for m in range(M_TILES):
             (nc.vector if m < 2 else nc.gpsimd).memset(window[m][:], 0.0)

@@ -34,7 +34,6 @@ def tile_routed_moe_kernel(tc, xT, w_words, w_scales, gate, offs, out):
         psum = ctx.enter_context(tc.psum_pool(name="psum", bufs=1))
 
         offsets = lists.tile([P, E * LIST_COLS], U16, name="offsets")
-        nc.sync.dma_start(offsets[:], offs)
 
         def expert_list(e):
             return offsets[:, LIST_COLS * e : LIST_COLS * (e + 1)]
@@ -92,6 +91,8 @@ def tile_routed_moe_kernel(tc, xT, w_words, w_scales, gate, offs, out):
 
         for i, (a, t) in enumerate(LOAD_ORDER):
             nc.sync.dma_start(plane[a, t][:], x_view[a, :, t, :])
+            if i == 0:
+                nc.sync.dma_start(offsets[:], offs)
             if i == 7:
                 load_scales()
         load_weights(0, 0, 2)

@@ -18,8 +18,7 @@ PACK = 4
 PASSES = K // (P * PACK)
 M_TILES = N // P
 LIST_COLS = C // 16
-SPLIT_BLOCKS = 2
-BACK_ORDER = tuple(range(SPLIT_BLOCKS, M_TILES)) + tuple(range(SPLIT_BLOCKS))
+HEAD = 128
 LOAD_ORDER = ((0, 0), (0, 2), (0, 1), (0, 3), (1, 0), (1, 2), (1, 1), (1, 3))
 
 
@@ -51,10 +50,10 @@ def tile_routed_moe_kernel(tc, xT, w_words, w_scales, gate, offs, out):
         x_scales = {}
         for a in range(PASSES):
             for e in range(E):
-                x_codes[a, e] = keep.tile([P, C], U32, name="xcodes%d%d" % (a, e), align_bytes=64)
+                x_codes[a, e] = keep.tile([P, C], U32, name="xcodes%d%d" % (a, e), tag="xcodes%d%d" % (a, e), align_bytes=64)
                 x_scales[a, e] = keep.tile([P, C], U8, name="xscales%d%d" % (a, e), align_bytes=64)
         w_planes = keep.tile([P, N], U8, name="w_planes", align_bytes=64)
-        w_codes = [keep.tile([P, N], U32, name="wcodes%d" % j, align_bytes=64) for j in range(E * PASSES)]
+        w_codes = keep.tile([P, E * PASSES, N], U32, name="w_codes", align_bytes=64)
         gate_sb = [keep.tile([P, E * C], F32, name="gate%d" % m) for m in range(M_TILES)]
         window = [keep.tile([P, T], F32, name="window%d" % m) for m in range(M_TILES)]
         sums = [keep.tile([P, E * C], F32, name="sums%d" % m) for m in range(M_TILES)]
@@ -69,7 +68,7 @@ def tile_routed_moe_kernel(tc, xT, w_words, w_scales, gate, offs, out):
             (nc.vector if m < 2 else nc.gpsimd).memset(window[m][:], 0.0)
 
         x_view = xT.rearrange("(a p t) n -> a p t n", p=P, t=PACK)
-        w_view = w_words.rearrange("e a p n r -> (e a) p (n r)")
+        w_view = w_words.rearrange("e a p n r -> e p a (n r)")
         s_view = w_scales.rearrange("e a q n -> (e a) q n")
 
         def load_scales():
@@ -80,11 +79,10 @@ def tile_routed_moe_kernel(tc, xT, w_words, w_scales, gate, offs, out):
                 )
 
         def load_weights(e, first, last):
-            for a in range(PASSES):
-                j = e * PASSES + a
-                nc.sync.dma_start(
-                    w_codes[j][:, P * first : P * last].bitcast(I32), w_view[j][:, PACK * P * first : PACK * P * last].bitcast(I32)
-                )
+            nc.sync.dma_start(
+                w_codes[:, e * PASSES : (e + 1) * PASSES, P * first : P * last].bitcast(I32),
+                w_view[e][:, :, PACK * P * first : PACK * P * last].bitcast(I32),
+            )
 
         def load_gate(m):
             nc.sync.dma_start(gate_sb[m][:], gate[P * m : P * (m + 1), :])
@@ -99,61 +97,93 @@ def tile_routed_moe_kernel(tc, xT, w_words, w_scales, gate, offs, out):
         load_gate(0)
         load_weights(0, 2, M_TILES)
         load_gate(1)
-        load_weights(1, 0, M_TILES)
         load_gate(2)
+        load_weights(1, 0, M_TILES)
         load_gate(3)
 
-        def quantise(a, e):
+        def quantise(a, first, last):
+            e = first // C
             nc.vector.quantize_mx(
-                out=x_codes[a, e][:].bitcast(FP8X4),
-                scales=x_scales[a, e][:],
-                in_=grouped[a][:, slots(e), :].rearrange("p c t -> p (c t)"),
+                out=x_codes[a, e][:, first - C * e : last - C * e].bitcast(FP8X4),
+                scales=x_scales[a, e][:, first - C * e : last - C * e],
+                in_=grouped[a][:, first:last, :].rearrange("p c t -> p (c t)"),
             )
 
-        for a, t in LOAD_ORDER:
+        def list_of(first, last):
+            return offsets[:, first // 16 : last // 16]
+
+        def scalar_gather(a, t, source, first, last):
+            nc.scalar.activation(grouped[a][:, first:last, t], source.indirect(list_of(first, last)), copy_fn)
+
+        def vector_gather(a, t, first, last):
+            nc.vector.tensor_copy(grouped[a][:, first:last, t], plane[a, t][:].indirect(list_of(first, last)))
+
+        for a, t in LOAD_ORDER[:-1]:
             if t < 2:
                 (nc.scalar.copy if (a, t) == (1, 0) else nc.vector.tensor_copy)(out=x_bf16[:, 2 * a + t, :], in_=plane[a, t][:])
-                for e in range(E):
-                    nc.scalar.activation(grouped[a][:, slots(e), t], x_bf16[:, 2 * a + t, :].indirect(expert_list(e)), copy_fn)
-            elif (a, t) != LOAD_ORDER[-1]:
+                pieces = ((0, HEAD), (HEAD, C), (C, E * C)) if (a, t) == (1, 1) else ((0, C), (C, E * C))
+                for first, last in pieces:
+                    scalar_gather(a, t, x_bf16[:, 2 * a + t, :], first, last)
+            else:
                 nc.vector.tensor_copy(grouped[a][:, :, t], plane[a, t][:].indirect(offsets[:]))
             if (a, t) == (0, 3):
-                quantise(0, 0)
-                quantise(0, 1)
+                quantise(0, 0, C)
+                quantise(0, C, E * C)
         a, t = LOAD_ORDER[-1]
-        for e in range(E):
-            nc.vector.tensor_copy(grouped[a][:, slots(e), t], plane[a, t][:].indirect(expert_list(e)))
-            quantise(1, e)
+        for first, last in ((0, HEAD), (HEAD, C)):
+            vector_gather(a, t, first, last)
+            quantise(a, first, last)
 
-        for e in range(E):
-            for m in (range(M_TILES) if e == 0 else BACK_ORDER):
-                acc = psum.tile([P, C], F32, name="acc%d%d" % (m, e))
-                for a in range(PASSES):
-                    j = e * PASSES + a
-                    nc.tensor.matmul_mx(
-                        out=acc[:],
-                        lhsT=w_codes[j][:, P * m : P * (m + 1)].bitcast(FP8X4),
-                        lhsT_scale=w_planes[4 * j : P, P * m : P * (m + 1)],
-                        rhs=x_codes[a, e][:].bitcast(FP8X4),
-                        rhs_scale=x_scales[a, e][:],
-                        start=(a == 0),
-                        stop=(a == PASSES - 1),
-                    )
-                nc.scalar.copy(out=sums[m][:, slots(e)], in_=acc[:])
+        def multiply(m, e, first, last, acc):
+            for a in range(PASSES):
+                j = e * PASSES + a
+                nc.tensor.matmul_mx(
+                    out=acc,
+                    lhsT=w_codes[:, j, P * m : P * (m + 1)].bitcast(FP8X4),
+                    lhsT_scale=w_planes[4 * j : P, P * m : P * (m + 1)],
+                    rhs=x_codes[a, e][:, first:last].bitcast(FP8X4),
+                    rhs_scale=x_scales[a, e][:, first:last],
+                    start=(a == 0),
+                    stop=(a == PASSES - 1),
+                )
 
-        def scatter_half(m, e):
-            nc.vector.tensor_tensor(
-                window[m][:].indirect(expert_list(e)), sums[m][:, slots(e)], gate_sb[m][:, slots(e)], mult
-            )
+        acc = {}
+
+        acc_head = psum.tile([P, HEAD], F32, name="acc_head", tag="acc31")
+        multiply(0, 0, 0, HEAD, acc_head[:])
+        nc.vector.tensor_copy(out=sums[0][:, 0:HEAD], in_=acc_head[:])
+        acc[0, 0] = psum.tile([P, C - HEAD], F32, name="acc00", tag="acc00")
+        multiply(0, 0, HEAD, C, acc[0, 0][:])
+        nc.scalar.copy(out=sums[0][:, HEAD:C], in_=acc[0, 0][:])
+        for m in range(1, M_TILES):
+            acc[m, 0] = psum.tile([P, C], F32, name="acc%d0" % m, tag="acc%d0" % m)
+            multiply(m, 0, 0, C, acc[m, 0][:])
+            if m < M_TILES - 1:
+                nc.scalar.copy(out=sums[m][:, slots(0)], in_=acc[m, 0][:])
+
+        last_bf16 = keep.tile([P, T], BF16, name="last_bf16", tag="xcodes10", align_bytes=64)
+        nc.scalar.copy(out=last_bf16[:], in_=plane[a, t][:])
+        scalar_gather(a, t, last_bf16[:], C, E * C)
+        nc.scalar.copy(out=sums[M_TILES - 1][:, slots(0)], in_=acc[M_TILES - 1, 0][:])
+
+        def scatter(m, first, last):
+            nc.vector.tensor_tensor(window[m][:].indirect(list_of(first, last)), sums[m][:, first:last], gate_sb[m][:, first:last], mult)
 
         def store(m):
             nc.sync.dma_start(out[P * m : P * (m + 1), :], window[m][:])
 
-        for m in range(SPLIT_BLOCKS):
-            scatter_half(m, 0)
-        for m in range(SPLIT_BLOCKS, M_TILES):
-            nc.vector.tensor_tensor(window[m][:].indirect(offsets[:]), sums[m][:], gate_sb[m][:], mult)
-            store(m)
-        for m in range(SPLIT_BLOCKS):
-            scatter_half(m, 1)
+        scatter(0, 0, HEAD)
+        scatter(0, HEAD, C)
+        for m in range(1, M_TILES - 1):
+            scatter(m, 0, C)
+
+        quantise(a, C, E * C)
+        for m in range(M_TILES):
+            acc[m, 1] = psum.tile([P, C], F32, name="acc%d1" % m, tag="acc%d1" % m)
+            multiply(m, 1, 0, C, acc[m, 1][:])
+            nc.scalar.copy(out=sums[m][:, slots(1)], in_=acc[m, 1][:])
+
+        scatter(M_TILES - 1, 0, C)
+        for m in range(M_TILES):
+            scatter(m, C, E * C)
             store(m)

@@ -120,7 +120,10 @@ def tile_routed_moe_kernel(tc, xT, w_words, w_scales, gate, offs, out):
 
         for a, t in LOAD_ORDER[:-1]:
             if t < 2:
-                (nc.scalar.copy if (a, t) == (1, 0) else nc.vector.tensor_copy)(out=x_bf16[:, 2 * a + t, :], in_=plane[a, t][:])
+                if (a, t) == (1, 1):
+                    nc.gpsimd.tensor_scalar(out=x_bf16[:, 2 * a + t, :], in0=plane[a, t][:], scalar1=1.0, scalar2=0.0, op0=mult, op1=mybir.AluOpType.add)
+                else:
+                    (nc.scalar.copy if (a, t) == (1, 0) else nc.vector.tensor_copy)(out=x_bf16[:, 2 * a + t, :], in_=plane[a, t][:])
                 pieces = ((0, HEAD), (HEAD, C), (C, E * C)) if (a, t) == (1, 1) else ((0, C), (C, E * C))
                 for first, last in pieces:
                     scalar_gather(a, t, x_bf16[:, 2 * a + t, :], first, last)

@@ -19,7 +19,7 @@ PASSES = K // (P * PACK)
 M_TILES = N // P
 LIST_COLS = C // 16
 HEAD = 128
-LOAD_ORDER = ((0, 0), (0, 2), (0, 1), (0, 3), (1, 0), (1, 2), (1, 1), (1, 3))
+LOAD_ORDER = ((0, 0), (0, 1), (0, 2), (0, 3), (1, 0), (1, 2), (1, 1), (1, 3))
 
 
 def tile_routed_moe_kernel(tc, xT, w_words, w_scales, gate, offs, out):

@@ -91,11 +91,10 @@ def tile_routed_moe_kernel(tc, xT, w_words, w_scales, gate, offs, out):
             nc.sync.dma_start(plane[a, t][:], x_view[a, :, t, :])
             if i == 0:
                 nc.sync.dma_start(offsets[:], offs)
-            if i == 7:
-                load_scales()
-        load_weights(0, 0, 2)
+        load_weights(0, 0, 1)
+        load_scales()
         load_gate(0)
-        load_weights(0, 2, M_TILES)
+        load_weights(0, 1, M_TILES)
         load_gate(1)
         load_gate(2)
         load_weights(1, 0, M_TILES)

@@ -48,10 +48,15 @@ def tile_routed_moe_kernel(tc, xT, w_words, w_scales, gate, offs, out):
         grouped = [keep.tile([P, E * C, PACK], BF16, name="grouped%d" % a, align_bytes=64) for a in range(PASSES)]
         x_codes = {}
         x_scales = {}
-        for a in range(PASSES):
-            for e in range(E):
-                x_codes[a, e] = keep.tile([P, C], U32, name="xcodes%d%d" % (a, e), tag="xcodes%d%d" % (a, e), align_bytes=64)
-                x_scales[a, e] = keep.tile([P, C], U8, name="xscales%d%d" % (a, e), align_bytes=64)
+        codes0 = keep.tile([P, E * C], U32, name="codes0", align_bytes=64)
+        scales0 = keep.tile([P, E * C], U8, name="scales0", align_bytes=64)
+        for e in range(E):
+            x_codes[0, e] = codes0[:, C * e : C * (e + 1)]
+            x_scales[0, e] = scales0[:, C * e : C * (e + 1)]
+            codes1 = keep.tile([P, C], U32, name="xcodes1%d" % e, tag="xcodes1%d" % e, align_bytes=64)
+            scales1 = keep.tile([P, C], U8, name="xscales1%d" % e, align_bytes=64)
+            x_codes[1, e] = codes1[:]
+            x_scales[1, e] = scales1[:]
         w_planes = keep.tile([P, N], U8, name="w_planes", align_bytes=64)
         w_codes = keep.tile([P, E * PASSES, N], U32, name="w_codes", align_bytes=64)
         gate_sb = [keep.tile([P, E * C], F32, name="gate%d" % m) for m in range(M_TILES)]
@@ -129,8 +134,11 @@ def tile_routed_moe_kernel(tc, xT, w_words, w_scales, gate, offs, out):
             else:
                 nc.vector.tensor_copy(grouped[a][:, :, t], plane[a, t][:].indirect(offsets[:]))
             if (a, t) == (0, 3):
-                quantise(0, 0, C)
-                quantise(0, C, E * C)
+                nc.vector.quantize_mx(
+                    out=codes0[:].bitcast(FP8X4),
+                    scales=scales0[:],
+                    in_=grouped[0][:].rearrange("p c t -> p (c t)"),
+                )
         a, t = LOAD_ORDER[-1]
         for first, last in ((0, HEAD), (HEAD, C)):
             vector_gather(a, t, first, last)

@@ -162,19 +162,19 @@ def tile_routed_moe_kernel(tc, xT, w_words, w_scales, gate, offs, out):
         acc_head = psum.tile([P, HEAD], F32, name="acc_head", tag="acc31")
         multiply(0, 0, 0, HEAD, acc_head[:])
         nc.vector.tensor_copy(out=sums[0][:, 0:HEAD], in_=acc_head[:])
-        acc[0, 0] = psum.tile([P, C - HEAD], F32, name="acc00", tag="acc00")
-        multiply(0, 0, HEAD, C, acc[0, 0][:])
-        nc.scalar.copy(out=sums[0][:, HEAD:C], in_=acc[0, 0][:])
         for m in range(1, M_TILES):
             acc[m, 0] = psum.tile([P, C], F32, name="acc%d0" % m, tag="acc%d0" % m)
             multiply(m, 0, 0, C, acc[m, 0][:])
             if m < M_TILES - 1:
                 nc.scalar.copy(out=sums[m][:, slots(0)], in_=acc[m, 0][:])
+        acc[0, 0] = psum.tile([P, C - HEAD], F32, name="acc00", tag="acc00")
+        multiply(0, 0, HEAD, C, acc[0, 0][:])
 
         last_bf16 = keep.tile([P, T], BF16, name="last_bf16", tag="xcodes10", align_bytes=64)
         nc.scalar.copy(out=last_bf16[:], in_=plane[a, t][:])
         scalar_gather(a, t, last_bf16[:], C, E * C)
         nc.scalar.copy(out=sums[M_TILES - 1][:, slots(0)], in_=acc[M_TILES - 1, 0][:])
+        nc.scalar.copy(out=sums[0][:, HEAD:C], in_=acc[0, 0][:])
 
         def scatter(m, first, last):
             nc.vector.tensor_tensor(window[m][:].indirect(list_of(first, last)), sums[m][:, first:last], gate_sb[m][:, first:last], mult)
@@ -183,7 +183,6 @@ def tile_routed_moe_kernel(tc, xT, w_words, w_scales, gate, offs, out):
             nc.sync.dma_start(out[P * m : P * (m + 1), :], window[m][:])
 
         scatter(0, 0, HEAD)
-        scatter(0, HEAD, C)
         for m in range(1, M_TILES - 1):
             scatter(m, 0, C)
 
@@ -195,5 +194,5 @@ def tile_routed_moe_kernel(tc, xT, w_words, w_scales, gate, offs, out):
 
         scatter(M_TILES - 1, 0, C)
         for m in range(M_TILES):
-            scatter(m, C, E * C)
+            scatter(m, HEAD if m == 0 else C, E * C)
             store(m)

@@ -161,7 +161,7 @@ def tile_routed_moe_kernel(tc, xT, w_words, w_scales, gate, offs, out):
 
         acc_head = psum.tile([P, HEAD], F32, name="acc_head", tag="acc31")
         multiply(0, 0, 0, HEAD, acc_head[:])
-        nc.vector.tensor_copy(out=sums[0][:, 0:HEAD], in_=acc_head[:])
+        nc.scalar.copy(out=sums[0][:, 0:HEAD], in_=acc_head[:])
         for m in range(1, M_TILES):
             acc[m, 0] = psum.tile([P, C], F32, name="acc%d0" % m, tag="acc%d0" % m)
             multiply(m, 0, 0, C, acc[m, 0][:])

@@ -96,11 +96,11 @@ def tile_routed_moe_kernel(tc, xT, w_words, w_scales, gate, offs, out):
             nc.sync.dma_start(plane[a, t][:], x_view[a, :, t, :])
             if i == 0:
                 nc.sync.dma_start(offsets[:], offs)
-        load_weights(0, 0, 1)
+        load_weights(0, 0, 2)
         load_scales()
         load_gate(0)
-        load_weights(0, 1, M_TILES)
         load_gate(1)
+        load_weights(0, 2, M_TILES)
         load_gate(2)
         load_weights(1, 0, M_TILES)
         load_gate(3)
@@ -162,18 +162,20 @@ def tile_routed_moe_kernel(tc, xT, w_words, w_scales, gate, offs, out):
         acc_head = psum.tile([P, HEAD], F32, name="acc_head", tag="acc31")
         multiply(0, 0, 0, HEAD, acc_head[:])
         nc.scalar.copy(out=sums[0][:, 0:HEAD], in_=acc_head[:])
+        acc[0, 0] = psum.tile([P, C - HEAD], F32, name="acc00", tag="acc00")
         for m in range(1, M_TILES):
+            if m == 2:
+                multiply(0, 0, HEAD, C, acc[0, 0][:])
             acc[m, 0] = psum.tile([P, C], F32, name="acc%d0" % m, tag="acc%d0" % m)
             multiply(m, 0, 0, C, acc[m, 0][:])
             if m < M_TILES - 1:
                 nc.scalar.copy(out=sums[m][:, slots(0)], in_=acc[m, 0][:])
-        acc[0, 0] = psum.tile([P, C - HEAD], F32, name="acc00", tag="acc00")
-        multiply(0, 0, HEAD, C, acc[0, 0][:])
 
         last_bf16 = keep.tile([P, T], BF16, name="last_bf16", tag="xcodes10", align_bytes=64)
         nc.scalar.copy(out=last_bf16[:], in_=plane[a, t][:])
         scalar_gather(a, t, last_bf16[:], C, E * C)
-        nc.scalar.copy(out=sums[M_TILES - 1][:, slots(0)], in_=acc[M_TILES - 1, 0][:])
+        sums_last = keep.tile([P, C], F32, name="sums_last", tag="xcodes10", align_bytes=64)
+        nc.scalar.copy(out=sums_last[:], in_=acc[M_TILES - 1, 0][:])
         nc.scalar.copy(out=sums[0][:, HEAD:C], in_=acc[0, 0][:])
 
         def scatter(m, first, last):
@@ -192,7 +194,7 @@ def tile_routed_moe_kernel(tc, xT, w_words, w_scales, gate, offs, out):
             multiply(m, 1, 0, C, acc[m, 1][:])
             nc.scalar.copy(out=sums[m][:, slots(1)], in_=acc[m, 1][:])
 
-        scatter(M_TILES - 1, 0, C)
+        nc.vector.tensor_tensor(window[M_TILES - 1][:].indirect(list_of(0, C)), sums_last[:], gate_sb[M_TILES - 1][:, 0:C], mult)
         for m in range(M_TILES):
             scatter(m, HEAD if m == 0 else C, E * C)
             store(m)

from contextlib import ExitStack

import concourse.mybir as mybir

K, T, E, C, N = 1024, 1024, 2, 256, 512
FLOPS = 2 * K * N * E * C

F32 = mybir.dt.float32
BF16 = mybir.dt.bfloat16
U32 = mybir.dt.uint32
I32 = mybir.dt.int32
U16 = mybir.dt.uint16
U8 = mybir.dt.uint8
FP8X4 = mybir.dt.float8_e4m3fn_x4

P = 128
PACK = 4
PASSES = K // (P * PACK)
M_TILES = N // P
LIST_COLS = C // 16
HEAD = 128
LOAD_ORDER = ((0, 0), (0, 1), (0, 2), (0, 3), (1, 0), (1, 2), (1, 1), (1, 3))


def tile_routed_moe_kernel(tc, xT, w_words, w_scales, gate, offs, out):
    nc = tc.nc
    mult = mybir.AluOpType.mult
    copy_fn = mybir.ActivationFunctionType.Copy

    with ExitStack() as ctx:
        lists = ctx.enter_context(tc.tile_pool(name="lists", bufs=1))
        keep = ctx.enter_context(tc.tile_pool(name="keep", bufs=1))
        psum = ctx.enter_context(tc.psum_pool(name="psum", bufs=1))

        offsets = lists.tile([P, E * LIST_COLS], U16, name="offsets")

        def expert_list(e):
            return offsets[:, LIST_COLS * e : LIST_COLS * (e + 1)]

        def slots(e):
            return slice(C * e, C * (e + 1))

        plane = {}
        for a in range(PASSES):
            for t in range(PACK):
                plane[a, t] = keep.tile([P, T], F32, name="plane%d%d" % (a, t))
        x_bf16 = keep.tile([P, PACK, T], BF16, name="x_bf16")
        grouped = [keep.tile([P, E * C, PACK], BF16, name="grouped%d" % a, align_bytes=64) for a in range(PASSES)]
        x_codes = {}
        x_scales = {}
        codes0 = keep.tile([P, E * C], U32, name="codes0", align_bytes=64)
        scales0 = keep.tile([P, E * C], U8, name="scales0", align_bytes=64)
        for e in range(E):
            x_codes[0, e] = codes0[:, C * e : C * (e + 1)]
            x_scales[0, e] = scales0[:, C * e : C * (e + 1)]
            codes1 = keep.tile([P, C], U32, name="xcodes1%d" % e, tag="xcodes1%d" % e, align_bytes=64)
            scales1 = keep.tile([P, C], U8, name="xscales1%d" % e, align_bytes=64)
            x_codes[1, e] = codes1[:]
            x_scales[1, e] = scales1[:]
        w_planes = keep.tile([P, N], U8, name="w_planes", align_bytes=64)
        w_codes = keep.tile([P, E * PASSES, N], U32, name="w_codes", align_bytes=64)
        gate_sb = [keep.tile([P, E * C], F32, name="gate%d" % m) for m in range(M_TILES)]
        window = [keep.tile([P, T], F32, name="window%d" % m) for m in range(M_TILES)]
        sums = [keep.tile([P, E * C], F32, name="sums%d" % m) for m in range(M_TILES)]

        warm_in = keep.tile([P, 1], F32, name="warm_in")
        warm_out = keep.tile([P, 1], F32, name="warm_out")
        nc.gpsimd.memset(warm_in[:], 0.0)
        nc.scalar.activation(warm_out[:], warm_in[:], copy_fn)

        nc.vector.memset(w_planes[:].bitcast(I32), 0)
        for m in range(M_TILES):
            (nc.vector if m < 2 else nc.gpsimd).memset(window[m][:], 0.0)

        x_view = xT.rearrange("(a p t) n -> a p t n", p=P, t=PACK)
        w_view = w_words.rearrange("e a p n r -> e p a (n r)")
        s_view = w_scales.rearrange("e a q n -> (e a) q n")

        def load_scales():
            for q in range(4):
                nc.sync.dma_start(
                    w_planes[32 * q : 32 * q + 16, :].bitcast(I32),
                    s_view[:, 4 * q : 4 * q + 4, :].bitcast(I32),
                )

        def load_weights(e, first, last):
            nc.sync.dma_start(
                w_codes[:, e * PASSES : (e + 1) * PASSES, P * first : P * last].bitcast(I32),
                w_view[e][:, :, PACK * P * first : PACK * P * last].bitcast(I32),
            )

        def load_gate(m):
            nc.sync.dma_start(gate_sb[m][:], gate[P * m : P * (m + 1), :])

        for i, (a, t) in enumerate(LOAD_ORDER):
            nc.sync.dma_start(plane[a, t][:], x_view[a, :, t, :])
            if i == 0:
                nc.sync.dma_start(offsets[:], offs)
        load_weights(0, 0, 2)
        load_scales()
        load_gate(0)
        load_gate(1)
        load_weights(0, 2, M_TILES)
        load_gate(2)
        load_weights(1, 0, M_TILES)
        load_gate(3)

        def quantise(a, first, last):
            e = first // C
            nc.vector.quantize_mx(
                out=x_codes[a, e][:, first - C * e : last - C * e].bitcast(FP8X4),
                scales=x_scales[a, e][:, first - C * e : last - C * e],
                in_=grouped[a][:, first:last, :].rearrange("p c t -> p (c t)"),
            )

        def list_of(first, last):
            return offsets[:, first // 16 : last // 16]

        def scalar_gather(a, t, source, first, last):
            nc.scalar.activation(grouped[a][:, first:last, t], source.indirect(list_of(first, last)), copy_fn)

        def vector_gather(a, t, first, last):
            nc.vector.tensor_copy(grouped[a][:, first:last, t], plane[a, t][:].indirect(list_of(first, last)))

        for a, t in LOAD_ORDER[:-1]:
            if t < 2:
                if (a, t) == (1, 1):
                    nc.gpsimd.tensor_scalar(out=x_bf16[:, 2 * a + t, :], in0=plane[a, t][:], scalar1=1.0, scalar2=0.0, op0=mult, op1=mybir.AluOpType.add)
                else:
                    (nc.scalar.copy if (a, t) == (1, 0) else nc.vector.tensor_copy)(out=x_bf16[:, 2 * a + t, :], in_=plane[a, t][:])
                pieces = ((0, HEAD), (HEAD, C), (C, E * C)) if (a, t) == (1, 1) else ((0, C), (C, E * C))
                for first, last in pieces:
                    scalar_gather(a, t, x_bf16[:, 2 * a + t, :], first, last)
            else:
                nc.vector.tensor_copy(grouped[a][:, :, t], plane[a, t][:].indirect(offsets[:]))
            if (a, t) == (0, 3):
                nc.vector.quantize_mx(
                    out=codes0[:].bitcast(FP8X4),
                    scales=scales0[:],
                    in_=grouped[0][:].rearrange("p c t -> p (c t)"),
                )
        a, t = LOAD_ORDER[-1]
        for first, last in ((0, HEAD), (HEAD, C)):
            vector_gather(a, t, first, last)
            quantise(a, first, last)

        def multiply(m, e, first, last, acc):
            for a in range(PASSES):
                j = e * PASSES + a
                nc.tensor.matmul_mx(
                    out=acc,
                    lhsT=w_codes[:, j, P * m : P * (m + 1)].bitcast(FP8X4),
                    lhsT_scale=w_planes[4 * j : P, P * m : P * (m + 1)],
                    rhs=x_codes[a, e][:, first:last].bitcast(FP8X4),
                    rhs_scale=x_scales[a, e][:, first:last],
                    start=(a == 0),
                    stop=(a == PASSES - 1),
                )

        acc = {}

        acc_head = psum.tile([P, HEAD], F32, name="acc_head", tag="acc31")
        multiply(0, 0, 0, HEAD, acc_head[:])
        nc.scalar.copy(out=sums[0][:, 0:HEAD], in_=acc_head[:])
        acc[0, 0] = psum.tile([P, C - HEAD], F32, name="acc00", tag="acc00")
        for m in range(1, M_TILES):
            if m == 2:
                multiply(0, 0, HEAD, C, acc[0, 0][:])
            acc[m, 0] = psum.tile([P, C], F32, name="acc%d0" % m, tag="acc%d0" % m)
            multiply(m, 0, 0, C, acc[m, 0][:])
            if m < M_TILES - 1:
                nc.scalar.copy(out=sums[m][:, slots(0)], in_=acc[m, 0][:])

        last_bf16 = keep.tile([P, T], BF16, name="last_bf16", tag="xcodes10", align_bytes=64)
        nc.scalar.copy(out=last_bf16[:], in_=plane[a, t][:])
        scalar_gather(a, t, last_bf16[:], C, E * C)
        sums_last = keep.tile([P, C], F32, name="sums_last", tag="xcodes10", align_bytes=64)
        nc.scalar.copy(out=sums_last[:], in_=acc[M_TILES - 1, 0][:])
        nc.scalar.copy(out=sums[0][:, HEAD:C], in_=acc[0, 0][:])

        def scatter(m, first, last):
            nc.vector.tensor_tensor(window[m][:].indirect(list_of(first, last)), sums[m][:, first:last], gate_sb[m][:, first:last], mult)

        def store(m):
            nc.sync.dma_start(out[P * m : P * (m + 1), :], window[m][:])

        scatter(0, 0, HEAD)
        for m in range(1, M_TILES - 1):
            scatter(m, 0, C)

        quantise(a, C, E * C)
        for m in range(M_TILES):
            acc[m, 1] = psum.tile([P, C], F32, name="acc%d1" % m, tag="acc%d1" % m)
            multiply(m, 1, 0, C, acc[m, 1][:])
            nc.scalar.copy(out=sums[m][:, slots(1)], in_=acc[m, 1][:])

        nc.vector.tensor_tensor(window[M_TILES - 1][:].indirect(list_of(0, C)), sums_last[:], gate_sb[M_TILES - 1][:, 0:C], mult)
        for m in range(M_TILES):
            scatter(m, HEAD if m == 0 else C, E * C)
            store(m)
